import numpy as np
import ml_dtypes


def mxq(x, axis, fmt="e4m3"):
    dtype, down = {"e4m3": (ml_dtypes.float8_e4m3fn, 7), "e5m2": (ml_dtypes.float8_e5m2, 14)}[fmt]
    v = np.moveaxis(np.asarray(x, np.float32).astype(ml_dtypes.bfloat16).astype(np.float64), axis, -1)
    blocks = v.reshape(v.shape[:-1] + (-1, 32))
    amax = np.abs(blocks).max(-1, keepdims=True)
    byte = np.maximum(np.where(amax > 0, np.frexp(amax)[1] - 1 + 127, 0) - down, 1)
    scale = np.exp2(byte - 127.0)
    codes = (blocks / scale).astype(np.float32).astype(dtype).astype(np.float64)
    return np.moveaxis((codes * scale).reshape(v.shape), -1, axis)


WIDE = False


def mx_kscale(k):
    if not WIDE:
        return np.ones(k)
    levels = np.array([10, -10, 5, -5, 0])
    if k % 512:
        return np.exp2(np.random.permutation(np.resize(levels, k // 32))).repeat(32)
    a = np.empty((k // 512, 16))
    for p in range(k // 512):
        a[p, :8] = np.random.permutation(np.resize(levels, 8))
        for g in range(8):
            far = levels[np.abs(levels - a[p, g]) >= 10]
            a[p, g + 8] = far[np.random.randint(len(far))]
    return np.exp2(a.ravel()).repeat(32)


def f64(x):
    return np.asarray(x).astype(np.float64)


def striped(idx):
    return np.tile(idx.reshape(-1, 16).T, (8, 1)).astype(np.uint16)


def unstriped(offs):
    return offs[:16].T.reshape(-1).astype(np.int64)


E2M1 = np.array([0.0, 0.5, 1.0, 1.5, 2.0, 3.0, 4.0, 6.0, -0.0, -0.5, -1.0, -1.5, -2.0, -3.0, -4.0, -6.0])


def pack_weight(w, fmt):
    k, n = w.shape
    w = f64(np.asarray(w, np.float32).astype(ml_dtypes.bfloat16)).reshape(k // 32, 32, n)
    amax = np.abs(w).max(1)
    if fmt == "e4m3":
        byte = np.frexp(amax)[1] - 1 + 127 - 7
    else:
        mant, ex = np.frexp(amax / 6.0)
        byte = np.where(mant > 0.5, ex, ex - 1) + 127
    byte = np.clip(np.where(amax > 0, byte, 1), 1, 254)
    scaled = (w * np.exp2(127.0 - byte)[:, None, :]).reshape(k, n).astype(np.float32)
    by_word = np.ascontiguousarray(scaled.reshape(k // 512, 128, 4, n).transpose(0, 1, 3, 2))
    if fmt == "e4m3":
        words = by_word.astype(ml_dtypes.float8_e4m3fn).view(np.uint8)
    else:
        c = by_word.astype(ml_dtypes.float4_e2m1fn).view(np.uint8) & 0xF
        words = (c[..., 0::2] | (c[..., 1::2] << 4)).reshape(k // 512, 128, 2 * n)
    return np.ascontiguousarray(words), np.ascontiguousarray(byte.astype(np.uint8).reshape(k // 512, 16, n))


def unpack_weight(words, scales, fmt):
    g, _, n = scales.shape
    words = np.ascontiguousarray(words).reshape(g, 128, n, -1)
    if fmt == "e4m3":
        vals = words.view(ml_dtypes.float8_e4m3fn).astype(np.float64)
    else:
        nib = np.empty((g, 128, n, 4), np.uint8)
        nib[..., 0::2] = words & 0xF
        nib[..., 1::2] = words >> 4
        vals = E2M1[nib]
    vals = vals * np.repeat(np.exp2(scales.astype(np.float64) - 127.0), 8, axis=1)[..., None]
    return vals.transpose(0, 1, 3, 2).reshape(g * 512, n)


def d_silu(v):
    s = 1.0 / (1.0 + np.exp(-np.maximum(v, -700.0)))
    return s * (1.0 + v * (1.0 - s))


K, T, E, C, H, N, TOP = 512, 512, 6, 256, 512, 1536, 3


def by_expert(wq, xq):
    return np.concatenate([wq[e].T @ xq[:, e * C:(e + 1) * C] for e in range(E)], axis=1)


def setup_inputs():
    n = np.random.standard_normal
    v = mx_kscale(N)
    u = mx_kscale(H)
    deal = np.repeat(np.arange(E), C).reshape(TOP, T)[:, np.random.permutation(T)]
    deal = np.take_along_axis(deal, np.argsort(np.random.rand(TOP, T), axis=0), axis=0)
    for _ in range(8):
        s_, t_ = np.random.permutation(T).reshape(2, -1); r = np.random.randint(TOP, size=T // 2); x, y = deal[r, s_].copy(), deal[r, t_].copy()
        ok = ~((deal[:, s_] == y).any(0) | (deal[:, t_] == x).any(0)); deal[r[ok], s_[ok]] = y[ok]; deal[r[ok], t_[ok]] = x[ok]
    order = np.lexsort((np.random.rand(TOP * T), deal.reshape(-1)))
    slot_token = order % T; pos = np.empty(TOP * T, np.int64); pos[order] = np.arange(TOP * T); pos = pos.reshape(TOP, T)
    g = np.random.uniform(0.5, 1.5, (TOP, T)); g = g / g.sum(0)
    w_slot = np.empty(E * C)
    for r in range(TOP): w_slot[pos[r]] = g[r]
    dy = pack_weight(n((N, T)) * v[:, None], "e4m3")
    w2t = pack_weight(n((N, H)) / np.sqrt(N) / v[:, None] * u, "e2m1")
    w1t = [pack_weight(m, "e2m1") for m in n((E, H, K)) / np.sqrt(H) / u[None, :, None]]
    return {
        "dy_words": dy[0],
        "dy_scales": dy[1],
        "w2t_words": w2t[0],
        "w2t_scales": w2t[1],
        "w1t_words": np.stack([m[0] for m in w1t]),
        "w1t_scales": np.stack([m[1] for m in w1t]),
        "a": (n((H, E * C))).astype(np.float32),
        "gate": (np.tile(w_slot, (128, 1))).astype(np.float32),
        "offs": striped(slot_token),
        "pos1": striped(pos[0]),
        "pos2": striped(pos[1]),
        "pos3": striped(pos[2]),
    }


def reference(dy_words, dy_scales, w2t_words, w2t_scales, w1t_words, w1t_scales, a, gate, offs, pos1, pos2, pos3):
    w2t = unpack_weight(w2t_words, w2t_scales, "e2m1")
    w1t = np.stack([unpack_weight(w1t_words[e], w1t_scales[e], "e2m1") for e in range(E)])
    idx = unstriped(offs)
    dc = w2t.T @ unpack_weight(dy_words, dy_scales, "e4m3")
    da = f64(gate[:1]) * dc[:, idx] * d_silu(f64(a))
    dx = by_expert(w1t, mxq(da, 0, "e4m3"))
    out = dx[:, unstriped(pos1)] + dx[:, unstriped(pos2)] + dx[:, unstriped(pos3)]
    return out

@@ -1,0 +1,228 @@
+from contextlib import ExitStack
+
+import concourse.mybir as mybir
+from concourse.masks import make_identity
+
+K, T, E, C, H, N, TOP = 512, 512, 6, 256, 512, 1536, 3
+S = E * C
+FLOPS = 2 * N * H * T + 2 * H * K * S
+
+F32 = mybir.dt.float32
+BF16 = mybir.dt.bfloat16
+I32 = mybir.dt.int32
+U32 = mybir.dt.uint32
+U16 = mybir.dt.uint16
+U8 = mybir.dt.uint8
+FP8X4 = mybir.dt.float8_e4m3fn_x4
+FP4X4 = mybir.dt.float4_e2m1fn_x4
+ACT = mybir.ActivationFunctionType
+ALU = mybir.AluOpType
+
+P = 128
+PACK = 4
+PASSES = N // (P * PACK)
+KT = K // P
+CHUNKS = [(0, 128), (128, 128), (256, 256), (512, 256), (768, 256), (1024, 256), (1280, 128), (1408, 128)]
+CAST_ON_SCALAR = [False] * 8
+
+
+def tile_moe_sdb_silu_kernel(
+    tc, dy_words, dy_scales, w2t_words, w2t_scales, w1t_words, w1t_scales, a, gate, offs, pos1, pos2, pos3, out
+):
+    nc = tc.nc
+    with ExitStack() as ctx:
+        lists = ctx.enter_context(tc.tile_pool(name="lists", bufs=1))
+        keep = ctx.enter_context(tc.tile_pool(name="keep", bufs=1))
+        ring = ctx.enter_context(tc.tile_pool(name="ring", bufs=3))
+        psum = ctx.enter_context(tc.psum_pool(name="psum", bufs=1))
+
+        def bank(b):
+            return psum.tile([P, 512], F32, name="bank%d" % b, tag="bank%d" % b)
+
+        def load_scale_rows(queue, plane, rows):
+            for q in range(4):
+                queue.dma_start(
+                    out=plane[32 * q : 32 * q + 4, :, :].bitcast(I32),
+                    in_=rows[:, 4 * q : 4 * q + 4, :].rearrange("s r n -> r s n").bitcast(I32),
+                )
+
+        w2_raw = keep.tile([P, PASSES, 2 * H], U8, name="w2_raw", align_bytes=64)
+        w2_scale_raw = keep.tile([P, PASSES, H], U8, name="w2_scale_raw", align_bytes=64)
+        w2 = keep.tile([P, PACK, PASSES, 2 * P], U8, name="w2", align_bytes=64)
+        w2_scale = keep.tile([P, PACK, PASSES, P], U8, name="w2_scale", align_bytes=64)
+        dy = keep.tile([P, PASSES, PACK * T], U8, name="dy", align_bytes=64)
+        dy_scale = keep.tile([P, PASSES, T], U8, name="dy_scale", align_bytes=64)
+        w1 = keep.tile([P, E, 2 * K], U8, name="w1", align_bytes=64)
+        w1_scale = keep.tile([P, E, K], U8, name="w1_scale", align_bytes=64)
+        gate_sb = keep.tile([P, S], F32, name="gate_sb")
+        a_sb = [keep.tile([P, PACK, n], F32, name="a%d" % c) for c, (s0, n) in enumerate(CHUNKS)]
+        dc = [keep.tile([P, T], F32, name="dc%d" % j) for j in range(PACK)]
+        codes = keep.tile([P, S], U32, name="codes", align_bytes=64)
+        code_scale = keep.tile([P, S], U8, name="code_scale", align_bytes=64)
+        dx = keep.tile([P, KT, S], F32, name="dx", align_bytes=64)
+        ident = keep.tile([P, P], F32, name="ident")
+        warm = keep.tile([P, 8], F32, name="warm")
+        warm_out = keep.tile([P, 8], F32, name="warm_out")
+        offs_sb = lists.tile([P, S // 16], U16, name="offs_sb")
+        pos_sb = [lists.tile([P, T // 16], U16, name="pos%d_sb" % r) for r in range(TOP)]
+
+        nc.vector.memset(w2_scale_raw[:].bitcast(I32), 0)
+        nc.vector.memset(dy_scale[:].bitcast(I32), 0)
+        nc.vector.memset(warm[:], 0.0)
+        nc.scalar.activation(warm_out[:], warm[:], ACT.Silu)
+        nc.vector.memset(w1_scale[:].bitcast(I32), 0)
+
+        a_rows = a.rearrange("(p j) s -> p j s", j=PACK)
+
+        def load_chunk(c):
+            s0, n = CHUNKS[c]
+            nc.sync.dma_start(out=a_sb[c][:], in_=a_rows[:, :, s0 : s0 + n])
+
+        def load_w1(e0, e1):
+            nc.sync.dma_start(
+                out=w1[:, e0:e1, :].bitcast(I32),
+                in_=w1t_words[e0:e1, 0].rearrange("e p b -> p e b").bitcast(I32),
+            )
+
+        nc.sync.dma_start(out=w2_raw[:].bitcast(I32), in_=w2t_words.rearrange("s p b -> p s b").bitcast(I32))
+        load_scale_rows(nc.sync, w2_scale_raw, w2t_scales)
+        for s in range(PASSES):
+            nc.sync.dma_start(
+                out=dy[:, s, :].bitcast(I32), in_=dy_words[s].rearrange("p t d -> p (t d)").bitcast(I32)
+            )
+        load_scale_rows(nc.sync, dy_scale, dy_scales)
+        load_chunk(0)
+        nc.sync.dma_start(out=gate_sb[:, 0:256], in_=gate[:, 0:256])
+        nc.sync.dma_start(offs_sb[:], offs)
+        load_chunk(1)
+        load_chunk(2)
+        nc.sync.dma_start(out=gate_sb[:, 256:S], in_=gate[:, 256:S])
+        load_scale_rows(nc.sync, w1_scale, w1t_scales[:, 0])
+        load_w1(0, 2)
+        load_chunk(3)
+        load_chunk(4)
+        load_w1(2, E)
+        for c in range(5, len(CHUNKS)):
+            load_chunk(c)
+        for r, pos in enumerate((pos1, pos2, pos3)):
+            nc.sync.dma_start(pos_sb[r][:], pos)
+        make_identity(nc, ident[:])
+
+        for j in range(PACK):
+            nc.vector.tensor_copy(
+                out=w2[:, j].bitcast(U16),
+                in_=w2_raw[:].bitcast(U16).rearrange("p s (m j) -> p j s m", j=PACK)[:, j],
+            )
+            nc.vector.tensor_copy(
+                out=w2_scale[:, j], in_=w2_scale_raw[:].rearrange("p s (m j) -> p j s m", j=PACK)[:, j]
+            )
+            acc = bank(j)
+            for s in range(PASSES):
+                nc.tensor.matmul_mx(
+                    out=acc[:],
+                    lhsT=w2[:, j, s, :].bitcast(FP4X4),
+                    lhsT_scale=w2_scale[:, j, s, :],
+                    rhs=dy[:, s, :].bitcast(FP8X4),
+                    rhs_scale=dy_scale[:, s, :],
+                    start=(s == 0),
+                    stop=(s == PASSES - 1),
+                )
+            nc.scalar.activation(dc[j][:], acc[:], ACT.Copy, scale=-0.5)
+
+        for c, (s0, n) in enumerate(CHUNKS):
+            e = s0 // C
+            slots = slice(s0, s0 + n)
+            th = ring.tile([P, PACK, n], F32, name="th", tag="th")
+            nc.scalar.activation(th[:], a_sb[c][:], ACT.Tanh, scale=0.5)
+            x = ring.tile([P, PACK, n], F32, name="x", tag="x")
+            nc.vector.scalar_tensor_tensor(
+                x[:], th[:], 1.0, gate_sb[:, slots].unsqueeze(1).to_broadcast([P, PACK, n]), ALU.add, ALU.mult
+            )
+            w = ring.tile([P, PACK * n], F32, name="w", tag="w")
+            g = ring.tile([P, PACK, n], F32, name="g", tag="g")
+            da = ring.tile([P, PACK * n], BF16, name="da", tag="da", align_bytes=64)
+            if CAST_ON_SCALAR[c]:
+                nc.scalar.activation(w[:], a_sb[c][:].rearrange("p j s -> p (j s)"), ACT.Silu, scale=-1.0)
+                f = ring.tile([P, PACK, n], F32, name="f", tag="f")
+                nc.vector.scalar_tensor_tensor(
+                    f[:].rearrange("p j s -> p (j s)"), w[:], -1.0, x[:].rearrange("p j s -> p (j s)"), ALU.add, ALU.mult
+                )
+            else:
+                nc.scalar.activation(
+                    w[:].rearrange("p (u i j) -> p u j i", i=4, j=PACK),
+                    a_sb[c][:].rearrange("p j (u i) -> p u j i", i=4),
+                    ACT.Silu,
+                    scale=-1.0,
+                )
+                f = x
+            for j in range(PACK):
+                nc.vector.tensor_tensor(
+                    g[:, j, :], dc[j][:].indirect(offs_sb[:, s0 // 16 : (s0 + n) // 16]), f[:, j, :], ALU.mult
+                )
+            if CAST_ON_SCALAR[c]:
+                nc.scalar.copy(
+                    da[:].rearrange("p (u i j) -> p u j i", i=4, j=PACK),
+                    g[:].rearrange("p j (u i) -> p u j i", i=4),
+                )
+            else:
+                nc.vector.scalar_tensor_tensor(
+                    da[:].rearrange("p (s j) -> p s j", j=PACK),
+                    w[:].rearrange("p (s j) -> p s j", j=PACK),
+                    -1.0,
+                    g[:].rearrange("p j s -> p s j"),
+                    ALU.add,
+                    ALU.mult,
+                )
+            nc.vector.quantize_mx(out=codes[:, slots].bitcast(FP8X4), scales=code_scale[:, slots], in_=da[:])
+            for half in range(2):
+                acc = bank(4 + 2 * (c % 2) + half)
+                for u in range(2):
+                    kt = 2 * half + u
+                    nc.tensor.matmul_mx(
+                        out=acc[:, u * n : (u + 1) * n],
+                        lhsT=w1[:, e, 2 * P * kt : 2 * P * (kt + 1)].bitcast(FP4X4),
+                        lhsT_scale=w1_scale[:, e, P * kt : P * (kt + 1)],
+                        rhs=codes[:, slots].bitcast(FP8X4),
+                        rhs_scale=code_scale[:, slots],
+                        start=True,
+                        stop=True,
+                    )
+                nc.scalar.copy(
+                    dx[:, 2 * half : 2 * half + 2, slots], acc[:, 0 : 2 * n].rearrange("p (u s) -> p u s", u=2)
+                )
+
+        for kt in range(KT):
+            got = [keep.tile([P, T], F32, name="got%d_%d" % (kt, r)) for r in range(TOP)]
+            res = keep.tile([P, T], F32, name="res%d" % kt)
+            if kt < KT - 1:
+                for r in range(TOP):
+                    nc.vector.tensor_copy(got[r][:], dx[:, kt, :].indirect(pos_sb[r][:]))
+                turned = bank(2 * (kt % 2))
+                for b in range(T // P):
+                    for r in range(TOP):
+                        nc.tensor.matmul(
+                            turned[:, b * P : (b + 1) * P],
+                            lhsT=got[r][:, b * P : (b + 1) * P],
+                            rhs=ident[:],
+                            start=(r == 0),
+                            stop=(r == TOP - 1),
+                            is_transpose=True,
+                        )
+                turned_sb = keep.tile([P, T], F32, name="turned%d" % kt)
+                nc.scalar.copy(turned_sb[:], turned[:])
+                back = bank(2 * (kt % 2) + 1)
+                for b in range(T // P):
+                    nc.tensor.transpose(back[:, b * P : (b + 1) * P], turned_sb[:, b * P : (b + 1) * P], ident[:])
+                nc.scalar.copy(res[:], back[:])
+                nc.sync.dma_start(out=out[kt * P : (kt + 1) * P, :], in_=res[:])
+            else:
+                pair = keep.tile([P, T], F32, name="pair")
+                for r in range(2):
+                    nc.vector.tensor_copy(got[r][:], dx[:, kt, :].indirect(pos_sb[r][:]))
+                halves = [slice(0, T // 2), slice(T // 2, T)]
+                nc.vector.tensor_copy(got[2][:, halves[0]], dx[:, kt, :].indirect(pos_sb[2][:, 0:16]))
+                nc.vector.tensor_tensor(pair[:], got[0][:], got[1][:], ALU.add)
+                nc.vector.tensor_copy(got[2][:, halves[1]], dx[:, kt, :].indirect(pos_sb[2][:, 16:32]))
+                for h in halves:
+                    nc.vector.tensor_tensor(res[:, h], pair[:, h], got[2][:, h], ALU.add)
+                    nc.sync.dma_start(out=out[kt * P : (kt + 1) * P, h], in_=res[:, h])

@@ -22,8 +22,7 @@ P = 128
 PACK = 4
 PASSES = N // (P * PACK)
 KT = K // P
-CHUNKS = [(0, 128), (128, 128), (256, 256), (512, 256), (768, 256), (1024, 256), (1280, 128), (1408, 128)]
-CAST_ON_SCALAR = [False] * 8
+CHUNKS = [(0, 256), (256, 256), (512, 256), (768, 256), (1024, 256), (1280, 128), (1408, 128)]
 
 
 def tile_moe_sdb_silu_kernel(
@@ -84,19 +83,23 @@ def tile_moe_sdb_silu_kernel(
                 in_=w1t_words[e0:e1, 0].rearrange("e p b -> p e b").bitcast(I32),
             )
 
-        nc.sync.dma_start(out=w2_raw[:].bitcast(I32), in_=w2t_words.rearrange("s p b -> p s b").bitcast(I32))
-        load_scale_rows(nc.sync, w2_scale_raw, w2t_scales)
-        for s in range(PASSES):
+        def load_dy(s):
             nc.sync.dma_start(
                 out=dy[:, s, :].bitcast(I32), in_=dy_words[s].rearrange("p t d -> p (t d)").bitcast(I32)
             )
-        load_scale_rows(nc.sync, dy_scale, dy_scales)
+
+        nc.sync.dma_start(out=w2_raw[:].bitcast(I32), in_=w2t_words.rearrange("s p b -> p s b").bitcast(I32))
+        load_scale_rows(nc.sync, w2_scale_raw, w2t_scales)
         load_chunk(0)
-        nc.sync.dma_start(out=gate_sb[:, 0:256], in_=gate[:, 0:256])
-        nc.sync.dma_start(offs_sb[:], offs)
+        nc.sync.dma_start(out=gate_sb[:, 0:C], in_=gate[:, 0:C])
+        load_dy(0)
+        load_scale_rows(nc.sync, dy_scale, dy_scales)
+        load_dy(1)
+        load_dy(2)
         load_chunk(1)
+        nc.sync.dma_start(offs_sb[:], offs)
+        nc.sync.dma_start(out=gate_sb[:, C:S], in_=gate[:, C:S])
         load_chunk(2)
-        nc.sync.dma_start(out=gate_sb[:, 256:S], in_=gate[:, 256:S])
         load_scale_rows(nc.sync, w1_scale, w1t_scales[:, 0])
         load_w1(0, 2)
         load_chunk(3)
@@ -129,51 +132,51 @@ def tile_moe_sdb_silu_kernel(
                 )
             nc.scalar.activation(dc[j][:], acc[:], ACT.Copy, scale=-0.5)
 
-        for c, (s0, n) in enumerate(CHUNKS):
+        last = len(CHUNKS) - 1
+        th, w, f, g, da = {}, {}, {}, {}, {}
+
+        def activations(c):
+            n = CHUNKS[c][1]
+            th[c] = ring.tile([P, PACK, n], F32, name="th", tag="th", bufs=4)
+            nc.scalar.activation(th[c][:], a_sb[c][:], ACT.Tanh, scale=0.5)
+            w[c] = ring.tile([P, PACK, n], F32, name="w", tag="w", bufs=4)
+            nc.scalar.activation(w[c][:], a_sb[c][:], ACT.Silu, scale=-1.0)
+
+        def gated(c):
+            s0, n = CHUNKS[c]
+            f[c] = ring.tile([P, PACK, n], F32, name="f", tag="f")
+            gates = gate_sb[:, s0 : s0 + n].unsqueeze(1).to_broadcast([P, PACK, n])
+            nc.vector.scalar_tensor_tensor(f[c][:], th[c][:], 1.0, gates, ALU.add, ALU.mult)
+
+        def factor(c):
+            nc.vector.scalar_tensor_tensor(f[c][:], w[c][:], -1.0, f[c][:], ALU.add, ALU.mult)
+
+        def gather(c, j):
+            s0, n = CHUNKS[c]
+            if j == 0:
+                g[c] = ring.tile([P, PACK, n], F32, name="g", tag="g")
+            window = dc[j][:].indirect(offs_sb[:, s0 // 16 : (s0 + n) // 16])
+            nc.vector.tensor_tensor(g[c][:, j, :], window, f[c][:, j, :], ALU.mult)
+
+        def interleave(c):
+            n = CHUNKS[c][1]
+            da[c] = ring.tile([P, PACK * n], BF16, name="da", tag="da", align_bytes=64)
+            copy = nc.vector.tensor_copy if c == last else nc.scalar.copy
+            copy(
+                da[c][:].rearrange("p (u i j) -> p u j i", i=4, j=PACK),
+                g[c][:].rearrange("p j (u i) -> p u j i", i=4),
+            )
+
+        def quantise(c):
+            s0, n = CHUNKS[c]
+            nc.vector.quantize_mx(
+                out=codes[:, s0 : s0 + n].bitcast(FP8X4), scales=code_scale[:, s0 : s0 + n], in_=da[c][:]
+            )
+
+        def expert(c):
+            s0, n = CHUNKS[c]
             e = s0 // C
             slots = slice(s0, s0 + n)
-            th = ring.tile([P, PACK, n], F32, name="th", tag="th")
-            nc.scalar.activation(th[:], a_sb[c][:], ACT.Tanh, scale=0.5)
-            x = ring.tile([P, PACK, n], F32, name="x", tag="x")
-            nc.vector.scalar_tensor_tensor(
-                x[:], th[:], 1.0, gate_sb[:, slots].unsqueeze(1).to_broadcast([P, PACK, n]), ALU.add, ALU.mult
-            )
-            w = ring.tile([P, PACK * n], F32, name="w", tag="w")
-            g = ring.tile([P, PACK, n], F32, name="g", tag="g")
-            da = ring.tile([P, PACK * n], BF16, name="da", tag="da", align_bytes=64)
-            if CAST_ON_SCALAR[c]:
-                nc.scalar.activation(w[:], a_sb[c][:].rearrange("p j s -> p (j s)"), ACT.Silu, scale=-1.0)
-                f = ring.tile([P, PACK, n], F32, name="f", tag="f")
-                nc.vector.scalar_tensor_tensor(
-                    f[:].rearrange("p j s -> p (j s)"), w[:], -1.0, x[:].rearrange("p j s -> p (j s)"), ALU.add, ALU.mult
-                )
-            else:
-                nc.scalar.activation(
-                    w[:].rearrange("p (u i j) -> p u j i", i=4, j=PACK),
-                    a_sb[c][:].rearrange("p j (u i) -> p u j i", i=4),
-                    ACT.Silu,
-                    scale=-1.0,
-                )
-                f = x
-            for j in range(PACK):
-                nc.vector.tensor_tensor(
-                    g[:, j, :], dc[j][:].indirect(offs_sb[:, s0 // 16 : (s0 + n) // 16]), f[:, j, :], ALU.mult
-                )
-            if CAST_ON_SCALAR[c]:
-                nc.scalar.copy(
-                    da[:].rearrange("p (u i j) -> p u j i", i=4, j=PACK),
-                    g[:].rearrange("p j (u i) -> p u j i", i=4),
-                )
-            else:
-                nc.vector.scalar_tensor_tensor(
-                    da[:].rearrange("p (s j) -> p s j", j=PACK),
-                    w[:].rearrange("p (s j) -> p s j", j=PACK),
-                    -1.0,
-                    g[:].rearrange("p j s -> p s j"),
-                    ALU.add,
-                    ALU.mult,
-                )
-            nc.vector.quantize_mx(out=codes[:, slots].bitcast(FP8X4), scales=code_scale[:, slots], in_=da[:])
             for half in range(2):
                 acc = bank(4 + 2 * (c % 2) + half)
                 for u in range(2):
@@ -187,9 +190,30 @@ def tile_moe_sdb_silu_kernel(
                         start=True,
                         stop=True,
                     )
-                nc.scalar.copy(
-                    dx[:, 2 * half : 2 * half + 2, slots], acc[:, 0 : 2 * n].rearrange("p (u s) -> p u s", u=2)
-                )
+                copy = nc.vector.tensor_copy if c == last and half == 0 else nc.scalar.copy
+                copy(dx[:, 2 * half : 2 * half + 2, slots], acc[:, 0 : 2 * n].rearrange("p (u s) -> p u s", u=2))
+
+        activations(0)
+        gated(0)
+        activations(1)
+        factor(0)
+        for c in range(last + 1):
+            if c + 2 <= last:
+                activations(c + 2)
+            gather(c, 0)
+            gather(c, 1)
+            if c < last:
+                gated(c + 1)
+            gather(c, 2)
+            if c > 0:
+                quantise(c - 1)
+                expert(c - 1)
+            if c < last:
+                factor(c + 1)
+            gather(c, 3)
+            interleave(c)
+        quantise(last)
+        expert(last)
 
         for kt in range(KT):
             got = [keep.tile([P, T], F32, name="got%d_%d" % (kt, r)) for r in range(TOP)]

@@ -23,6 +23,8 @@ PACK = 4
 PASSES = N // (P * PACK)
 KT = K // P
 CHUNKS = [(0, 256), (256, 256), (512, 256), (768, 256), (1024, 256), (1280, 128), (1408, 128)]
+GATED_ON_SCALAR = ()
+DIRECT = 2
 
 
 def tile_moe_sdb_silu_kernel(
@@ -47,13 +49,15 @@ def tile_moe_sdb_silu_kernel(
 
         w2_raw = keep.tile([P, PASSES, 2 * H], U8, name="w2_raw", align_bytes=64)
         w2_scale_raw = keep.tile([P, PASSES, H], U8, name="w2_scale_raw", align_bytes=64)
-        w2 = keep.tile([P, PACK, PASSES, 2 * P], U8, name="w2", align_bytes=64)
-        w2_scale = keep.tile([P, PACK, PASSES, P], U8, name="w2_scale", align_bytes=64)
+        w2 = keep.tile([P, PASSES, PACK, 2 * P], U8, name="w2", align_bytes=64)
+        w2_scale = keep.tile([P, PASSES, PACK, P], U8, name="w2_scale", align_bytes=64)
         dy = keep.tile([P, PASSES, PACK * T], U8, name="dy", align_bytes=64)
         dy_scale = keep.tile([P, PASSES, T], U8, name="dy_scale", align_bytes=64)
         w1 = keep.tile([P, E, 2 * K], U8, name="w1", align_bytes=64)
         w1_scale = keep.tile([P, E, K], U8, name="w1_scale", align_bytes=64)
-        gate_sb = keep.tile([P, S], F32, name="gate_sb")
+        gate_sb = keep.tile([P, DIRECT * C], F32, name="gate_sb")
+        gate_rows = keep.tile([P, P], F32, name="gate_rows")
+        gate_cols = keep.tile([P, S // P], F32, name="gate_cols")
         a_sb = [keep.tile([P, PACK, n], F32, name="a%d" % c) for c, (s0, n) in enumerate(CHUNKS)]
         dc = [keep.tile([P, T], F32, name="dc%d" % j) for j in range(PACK)]
         codes = keep.tile([P, S], U32, name="codes", align_bytes=64)
@@ -65,11 +69,11 @@ def tile_moe_sdb_silu_kernel(
         offs_sb = lists.tile([P, S // 16], U16, name="offs_sb")
         pos_sb = [lists.tile([P, T // 16], U16, name="pos%d_sb" % r) for r in range(TOP)]
 
-        nc.vector.memset(w2_scale_raw[:].bitcast(I32), 0)
+        nc.gpsimd.memset(w2_scale_raw[:].bitcast(I32), 0)
         nc.vector.memset(dy_scale[:].bitcast(I32), 0)
         nc.vector.memset(warm[:], 0.0)
         nc.scalar.activation(warm_out[:], warm[:], ACT.Silu)
-        nc.vector.memset(w1_scale[:].bitcast(I32), 0)
+        nc.gpsimd.memset(w1_scale[:].bitcast(I32), 0)
 
         a_rows = a.rearrange("(p j) s -> p j s", j=PACK)
 
@@ -83,23 +87,26 @@ def tile_moe_sdb_silu_kernel(
                 in_=w1t_words[e0:e1, 0].rearrange("e p b -> p e b").bitcast(I32),
             )
 
-        def load_dy(s):
+        def load_w2(s0, s1):
+            nc.sync.dma_start(
+                out=w2_raw[:, s0:s1, :].bitcast(I32), in_=w2t_words[s0:s1].rearrange("s p b -> p s b").bitcast(I32)
+            )
+
+        load_w2(0, 1)
+        load_scale_rows(nc.sync, w2_scale_raw, w2t_scales)
+        load_w2(1, PASSES)
+        load_chunk(0)
+        nc.sync.dma_start(out=gate_sb[:, 0:C], in_=gate[:, 0:C])
+        load_scale_rows(nc.sync, dy_scale, dy_scales)
+        for s in range(PASSES):
             nc.sync.dma_start(
                 out=dy[:, s, :].bitcast(I32), in_=dy_words[s].rearrange("p t d -> p (t d)").bitcast(I32)
             )
-
-        nc.sync.dma_start(out=w2_raw[:].bitcast(I32), in_=w2t_words.rearrange("s p b -> p s b").bitcast(I32))
-        load_scale_rows(nc.sync, w2_scale_raw, w2t_scales)
-        load_chunk(0)
-        nc.sync.dma_start(out=gate_sb[:, 0:C], in_=gate[:, 0:C])
-        load_dy(0)
-        load_scale_rows(nc.sync, dy_scale, dy_scales)
-        load_dy(1)
-        load_dy(2)
         load_chunk(1)
+        nc.sync.dma_start(out=gate_sb[:, C : 2 * C], in_=gate[:, C : 2 * C])
         nc.sync.dma_start(offs_sb[:], offs)
-        nc.sync.dma_start(out=gate_sb[:, C:S], in_=gate[:, C:S])
         load_chunk(2)
+        nc.sync.dma_start(out=gate_rows[:], in_=gate.rearrange("r (b c) -> (r b) c", c=P)[0:P, :])
         load_scale_rows(nc.sync, w1_scale, w1t_scales[:, 0])
         load_w1(0, 2)
         load_chunk(3)
@@ -111,20 +118,25 @@ def tile_moe_sdb_silu_kernel(
             nc.sync.dma_start(pos_sb[r][:], pos)
         make_identity(nc, ident[:])
 
+        def permute_words(s0, s1):
+            nc.vector.tensor_copy(
+                out=w2[:, s0:s1].bitcast(U16),
+                in_=w2_raw[:, s0:s1].bitcast(U16).rearrange("p s (m j) -> p s j m", j=PACK),
+            )
+
+        permute_words(0, 1)
+        nc.vector.tensor_copy(
+            out=w2_scale[:].rearrange("p s j m -> p j s m"),
+            in_=w2_scale_raw[:].rearrange("p s (m j) -> p j s m", j=PACK),
+        )
+        permute_words(1, PASSES)
         for j in range(PACK):
-            nc.vector.tensor_copy(
-                out=w2[:, j].bitcast(U16),
-                in_=w2_raw[:].bitcast(U16).rearrange("p s (m j) -> p j s m", j=PACK)[:, j],
-            )
-            nc.vector.tensor_copy(
-                out=w2_scale[:, j], in_=w2_scale_raw[:].rearrange("p s (m j) -> p j s m", j=PACK)[:, j]
-            )
             acc = bank(j)
             for s in range(PASSES):
                 nc.tensor.matmul_mx(
                     out=acc[:],
-                    lhsT=w2[:, j, s, :].bitcast(FP4X4),
-                    lhsT_scale=w2_scale[:, j, s, :],
+                    lhsT=w2[:, s, j, :].bitcast(FP4X4),
+                    lhsT_scale=w2_scale[:, s, j, :],
                     rhs=dy[:, s, :].bitcast(FP8X4),
                     rhs_scale=dy_scale[:, s, :],
                     start=(s == 0),
@@ -133,28 +145,65 @@ def tile_moe_sdb_silu_kernel(
             nc.scalar.activation(dc[j][:], acc[:], ACT.Copy, scale=-0.5)
 
         last = len(CHUNKS) - 1
-        th, w, f, g, da = {}, {}, {}, {}, {}
+        th, x, w, f, g, da = {}, {}, {}, {}, {}, {}
 
-        def activations(c):
-            n = CHUNKS[c][1]
-            th[c] = ring.tile([P, PACK, n], F32, name="th", tag="th", bufs=4)
-            nc.scalar.activation(th[c][:], a_sb[c][:], ACT.Tanh, scale=0.5)
-            w[c] = ring.tile([P, PACK, n], F32, name="w", tag="w", bufs=4)
-            nc.scalar.activation(w[c][:], a_sb[c][:], ACT.Silu, scale=-1.0)
+        gate_turned = bank(6)
+        nc.tensor.transpose(gate_turned[:, 0:P], gate_rows[:], ident[:])
+        nc.scalar.copy(gate_cols[:], gate_turned[:, 0 : S // P])
 
-        def gated(c):
+        def blocks(c):
             s0, n = CHUNKS[c]
-            f[c] = ring.tile([P, PACK, n], F32, name="f", tag="f")
-            gates = gate_sb[:, s0 : s0 + n].unsqueeze(1).to_broadcast([P, PACK, n])
-            nc.vector.scalar_tensor_tensor(f[c][:], th[c][:], 1.0, gates, ALU.add, ALU.mult)
+            return range(s0 // P, (s0 + n) // P)
 
-        def factor(c):
-            nc.vector.scalar_tensor_tensor(f[c][:], w[c][:], -1.0, f[c][:], ALU.add, ALU.mult)
+        def columns(c, b):
+            return slice(b * P - CHUNKS[c][0], (b + 1) * P - CHUNKS[c][0])
+
+        def silu(c):
+            w[c] = keep.tile([P, PACK, CHUNKS[c][1]], F32, name="silu%d" % c)
+            nc.scalar.activation(w[c][:], a_sb[c][:], ACT.Silu, scale=-1.0)
+            f[c] = ring.tile([P, PACK, CHUNKS[c][1]], F32, name="f", tag="f", bufs=2)
+
+        def tanh_turned(c):
+            for b in blocks(c):
+                turned = bank(4 + b % 2)
+                for j in range(PACK):
+                    nc.tensor.transpose(turned[:, j * P : (j + 1) * P], a_sb[c][:, j, columns(c, b)], ident[:])
+                th[b] = keep.tile([P, H], F32, name="th%d" % b)
+                nc.scalar.activation(th[b][:], turned[:], ACT.Tanh, scale=0.5)
+
+        def gated(c, b):
+            col = gate_cols[:, b : b + 1]
+            y = ring.tile([P, H], F32, name="y", tag="y", bufs=2)
+            if c in GATED_ON_SCALAR:
+                nc.scalar.activation(y[:], th[b][:], ACT.Identity, bias=col, scale=col)
+            else:
+                nc.vector.tensor_scalar(y[:], th[b][:], col, col, ALU.mult, ALU.add)
+            x[b] = bank(6 + b % 2)
+            for j in range(PACK):
+                nc.tensor.transpose(x[b][:, j * P : (j + 1) * P], y[:, j * P : (j + 1) * P], ident[:])
+
+        def factor(c, b):
+            cols = columns(c, b)
+            nc.vector.scalar_tensor_tensor(
+                f[c][:, :, cols], w[c][:, :, cols], -1.0, x[b][:].rearrange("p (j s) -> p j s", j=PACK), ALU.add, ALU.mult
+            )
+
+        def direct_activations(c):
+            th[c, "direct"] = keep.tile([P, PACK, C], F32, name="th_direct%d" % c)
+            nc.scalar.activation(th[c, "direct"][:], a_sb[c][:], ACT.Tanh, scale=0.5)
+            silu(c)
+
+        def direct_gated(c):
+            gates = gate_sb[:, c * C : (c + 1) * C].unsqueeze(1).to_broadcast([P, PACK, C])
+            nc.vector.scalar_tensor_tensor(th[c, "direct"][:], th[c, "direct"][:], 1.0, gates, ALU.add, ALU.mult)
+
+        def direct_factor(c):
+            nc.vector.scalar_tensor_tensor(f[c][:], w[c][:], -1.0, th[c, "direct"][:], ALU.add, ALU.mult)
 
         def gather(c, j):
             s0, n = CHUNKS[c]
             if j == 0:
-                g[c] = ring.tile([P, PACK, n], F32, name="g", tag="g")
+                g[c] = ring.tile([P, PACK, n], F32, name="g", tag="g", bufs=2)
             window = dc[j][:].indirect(offs_sb[:, s0 // 16 : (s0 + n) // 16])
             nc.vector.tensor_tensor(g[c][:, j, :], window, f[c][:, j, :], ALU.mult)
 
@@ -178,7 +227,7 @@ def tile_moe_sdb_silu_kernel(
             e = s0 // C
             slots = slice(s0, s0 + n)
             for half in range(2):
-                acc = bank(4 + 2 * (c % 2) + half)
+                acc = bank(2 * (c % 2) + half)
                 for u in range(2):
                     kt = 2 * half + u
                     nc.tensor.matmul_mx(
@@ -193,23 +242,35 @@ def tile_moe_sdb_silu_kernel(
                 copy = nc.vector.tensor_copy if c == last and half == 0 else nc.scalar.copy
                 copy(dx[:, 2 * half : 2 * half + 2, slots], acc[:, 0 : 2 * n].rearrange("p (u s) -> p u s", u=2))
 
-        activations(0)
-        gated(0)
-        activations(1)
-        factor(0)
+        direct_activations(0)
+        direct_gated(0)
+        direct_activations(1)
+        direct_factor(0)
+        direct_gated(1)
+        tanh_turned(2)
         for c in range(last + 1):
+            ahead = list(blocks(c + 1)) if DIRECT <= c + 1 <= last else []
+            two_ahead = list(blocks(c + 2)) if c + 2 <= last else []
             if c + 2 <= last:
-                activations(c + 2)
+                silu(c + 2)
+            if c + 3 <= last:
+                tanh_turned(c + 3)
             gather(c, 0)
+            if c == 0:
+                direct_factor(1)
+            for b in ahead[:1]:
+                factor(c + 1, b)
             gather(c, 1)
-            if c < last:
-                gated(c + 1)
-            gather(c, 2)
+            for b in two_ahead[:1]:
+                gated(c + 2, b)
             if c > 0:
                 quantise(c - 1)
                 expert(c - 1)
-            if c < last:
-                factor(c + 1)
+            gather(c, 2)
+            for b in ahead[1:]:
+                factor(c + 1, b)
+            for b in two_ahead[1:]:
+                gated(c + 2, b)
             gather(c, 3)
             interleave(c)
         quantise(last)
@@ -219,13 +280,12 @@ def tile_moe_sdb_silu_kernel(
             got = [keep.tile([P, T], F32, name="got%d_%d" % (kt, r)) for r in range(TOP)]
             res = keep.tile([P, T], F32, name="res%d" % kt)
             if kt < KT - 1:
+                turned = [bank(b) for b in range(T // P)]
                 for r in range(TOP):
                     nc.vector.tensor_copy(got[r][:], dx[:, kt, :].indirect(pos_sb[r][:]))
-                turned = bank(2 * (kt % 2))
-                for b in range(T // P):
-                    for r in range(TOP):
+                    for b in range(T // P):
                         nc.tensor.matmul(
-                            turned[:, b * P : (b + 1) * P],
+                            turned[b][:, 0:P],
                             lhsT=got[r][:, b * P : (b + 1) * P],
                             rhs=ident[:],
                             start=(r == 0),
@@ -233,9 +293,9 @@ def tile_moe_sdb_silu_kernel(
                             is_transpose=True,
                         )
                 turned_sb = keep.tile([P, T], F32, name="turned%d" % kt)
-                nc.scalar.copy(turned_sb[:], turned[:])
-                back = bank(2 * (kt % 2) + 1)
+                back = bank(4 + kt % 2)
                 for b in range(T // P):
+                    nc.scalar.copy(turned_sb[:, b * P : (b + 1) * P], turned[b][:, 0:P])
                     nc.tensor.transpose(back[:, b * P : (b + 1) * P], turned_sb[:, b * P : (b + 1) * P], ident[:])
                 nc.scalar.copy(res[:], back[:])
                 nc.sync.dma_start(out=out[kt * P : (kt + 1) * P, :], in_=res[:])

@@ -23,8 +23,10 @@ PACK = 4
 PASSES = N // (P * PACK)
 KT = K // P
 CHUNKS = [(0, 256), (256, 256), (512, 256), (768, 256), (1024, 256), (1280, 128), (1408, 128)]
-GATED_ON_SCALAR = ()
-DIRECT = 2
+GATED_ON_SCALAR = (3, 4, 5)
+DIRECT = 3
+EARLY = 1
+CAST_ON_VECTOR = (6,)
 
 
 def tile_moe_sdb_silu_kernel(
@@ -92,28 +94,35 @@ def tile_moe_sdb_silu_kernel(
                 out=w2_raw[:, s0:s1, :].bitcast(I32), in_=w2t_words[s0:s1].rearrange("s p b -> p s b").bitcast(I32)
             )
 
-        load_w2(0, 1)
-        load_scale_rows(nc.sync, w2_scale_raw, w2t_scales)
+        def load_dy(s0, s1):
+            nc.sync.dma_start(
+                out=dy[:, s0:s1, :].bitcast(I32),
+                in_=dy_words[s0:s1].rearrange("s p t d -> p s (t d)").bitcast(I32),
+            )
+
+        def load_gate(c0, c1):
+            nc.sync.dma_start(out=gate_sb[:, c0 * C : c1 * C], in_=gate[:, c0 * C : c1 * C])
+
         load_w2(1, PASSES)
         load_chunk(0)
-        nc.sync.dma_start(out=gate_sb[:, 0:C], in_=gate[:, 0:C])
-        load_scale_rows(nc.sync, dy_scale, dy_scales)
-        for s in range(PASSES):
-            nc.sync.dma_start(
-                out=dy[:, s, :].bitcast(I32), in_=dy_words[s].rearrange("p t d -> p (t d)").bitcast(I32)
-            )
+        load_w2(0, 1)
+        load_scale_rows(nc.sync, w2_scale_raw, w2t_scales)
+        load_gate(0, 1)
         load_chunk(1)
-        nc.sync.dma_start(out=gate_sb[:, C : 2 * C], in_=gate[:, C : 2 * C])
-        nc.sync.dma_start(offs_sb[:], offs)
+        load_dy(0, 1)
+        load_scale_rows(nc.sync, dy_scale, dy_scales)
+        load_gate(1, DIRECT)
         load_chunk(2)
+        load_dy(1, 2)
+        load_dy(2, 3)
+        nc.sync.dma_start(offs_sb[:], offs)
         nc.sync.dma_start(out=gate_rows[:], in_=gate.rearrange("r (b c) -> (r b) c", c=P)[0:P, :])
-        load_scale_rows(nc.sync, w1_scale, w1t_scales[:, 0])
-        load_w1(0, 2)
         load_chunk(3)
         load_chunk(4)
-        load_w1(2, E)
-        for c in range(5, len(CHUNKS)):
-            load_chunk(c)
+        load_w1(0, E)
+        load_chunk(5)
+        load_chunk(6)
+        load_scale_rows(nc.sync, w1_scale, w1t_scales[:, 0])
         for r, pos in enumerate((pos1, pos2, pos3)):
             nc.sync.dma_start(pos_sb[r][:], pos)
         make_identity(nc, ident[:])
@@ -132,20 +141,21 @@ def tile_moe_sdb_silu_kernel(
         permute_words(1, PASSES)
         for j in range(PACK):
             acc = bank(j)
-            for s in range(PASSES):
+            order = [0, 1, 2] if j == 0 else [2, 0, 1]
+            for s in order:
                 nc.tensor.matmul_mx(
                     out=acc[:],
                     lhsT=w2[:, s, j, :].bitcast(FP4X4),
                     lhsT_scale=w2_scale[:, s, j, :],
                     rhs=dy[:, s, :].bitcast(FP8X4),
                     rhs_scale=dy_scale[:, s, :],
-                    start=(s == 0),
-                    stop=(s == PASSES - 1),
+                    start=(s == order[0]),
+                    stop=(s == order[-1]),
                 )
             nc.scalar.activation(dc[j][:], acc[:], ACT.Copy, scale=-0.5)
 
         last = len(CHUNKS) - 1
-        th, x, w, f, g, da = {}, {}, {}, {}, {}, {}
+        th, x, w, f, g, da, sums = {}, {}, {}, {}, {}, {}, {}
 
         gate_turned = bank(6)
         nc.tensor.transpose(gate_turned[:, 0:P], gate_rows[:], ident[:])
@@ -173,7 +183,7 @@ def tile_moe_sdb_silu_kernel(
 
         def gated(c, b):
             col = gate_cols[:, b : b + 1]
-            y = ring.tile([P, H], F32, name="y", tag="y", bufs=2)
+            y = ring.tile([P, H], F32, name="y", tag="y", bufs=3)
             if c in GATED_ON_SCALAR:
                 nc.scalar.activation(y[:], th[b][:], ACT.Identity, bias=col, scale=col)
             else:
@@ -203,14 +213,14 @@ def tile_moe_sdb_silu_kernel(
         def gather(c, j):
             s0, n = CHUNKS[c]
             if j == 0:
-                g[c] = ring.tile([P, PACK, n], F32, name="g", tag="g", bufs=2)
+                g[c] = ring.tile([P, PACK, n], F32, name="g", tag="g", bufs=4)
             window = dc[j][:].indirect(offs_sb[:, s0 // 16 : (s0 + n) // 16])
             nc.vector.tensor_tensor(g[c][:, j, :], window, f[c][:, j, :], ALU.mult)
 
         def interleave(c):
             n = CHUNKS[c][1]
             da[c] = ring.tile([P, PACK * n], BF16, name="da", tag="da", align_bytes=64)
-            copy = nc.vector.tensor_copy if c == last else nc.scalar.copy
+            copy = nc.vector.tensor_copy if c in CAST_ON_VECTOR else nc.scalar.copy
             copy(
                 da[c][:].rearrange("p (u i j) -> p u j i", i=4, j=PACK),
                 g[c][:].rearrange("p j (u i) -> p u j i", i=4),
@@ -222,65 +232,93 @@ def tile_moe_sdb_silu_kernel(
                 out=codes[:, s0 : s0 + n].bitcast(FP8X4), scales=code_scale[:, s0 : s0 + n], in_=da[c][:]
             )
 
+        def product(acc, kt, s0, n):
+            e = s0 // C
+            nc.tensor.matmul_mx(
+                out=acc,
+                lhsT=w1[:, e, 2 * P * kt : 2 * P * (kt + 1)].bitcast(FP4X4),
+                lhsT_scale=w1_scale[:, e, P * kt : P * (kt + 1)],
+                rhs=codes[:, s0 : s0 + n].bitcast(FP8X4),
+                rhs_scale=code_scale[:, s0 : s0 + n],
+                start=True,
+                stop=True,
+            )
+
         def expert(c):
             s0, n = CHUNKS[c]
-            e = s0 // C
-            slots = slice(s0, s0 + n)
-            for half in range(2):
-                acc = bank(2 * (c % 2) + half)
-                for u in range(2):
-                    kt = 2 * half + u
-                    nc.tensor.matmul_mx(
-                        out=acc[:, u * n : (u + 1) * n],
-                        lhsT=w1[:, e, 2 * P * kt : 2 * P * (kt + 1)].bitcast(FP4X4),
-                        lhsT_scale=w1_scale[:, e, P * kt : P * (kt + 1)],
-                        rhs=codes[:, slots].bitcast(FP8X4),
-                        rhs_scale=code_scale[:, slots],
-                        start=True,
-                        stop=True,
-                    )
-                copy = nc.vector.tensor_copy if c == last and half == 0 else nc.scalar.copy
-                copy(dx[:, 2 * half : 2 * half + 2, slots], acc[:, 0 : 2 * n].rearrange("p (u s) -> p u s", u=2))
+            sums[c] = bank(c % 2)
+            for kt in range(EARLY):
+                product(sums[c][:, kt * n : (kt + 1) * n], kt, s0, n)
 
-        direct_activations(0)
-        direct_gated(0)
-        direct_activations(1)
-        direct_factor(0)
-        direct_gated(1)
-        tanh_turned(2)
-        for c in range(last + 1):
-            ahead = list(blocks(c + 1)) if DIRECT <= c + 1 <= last else []
-            two_ahead = list(blocks(c + 2)) if c + 2 <= last else []
-            if c + 2 <= last:
-                silu(c + 2)
-            if c + 3 <= last:
-                tanh_turned(c + 3)
-            gather(c, 0)
-            if c == 0:
-                direct_factor(1)
-            for b in ahead[:1]:
-                factor(c + 1, b)
-            gather(c, 1)
-            for b in two_ahead[:1]:
-                gated(c + 2, b)
+        def collect(c):
+            s0, n = CHUNKS[c]
+            copy = nc.vector.tensor_copy if c == last else nc.scalar.copy
+            copy(dx[:, 0:EARLY, s0 : s0 + n], sums[c][:, 0 : EARLY * n].rearrange("p (u s) -> p u s", u=EARLY))
+
+        def later_rows(kt):
+            for pair in range(E // 2):
+                acc = bank([2, 3, 6, 7][(3 * kt + pair) % len([2, 3, 6, 7])])
+                for u in range(2):
+                    product(acc[:, u * C : (u + 1) * C], kt, (2 * pair + u) * C, C)
+                nc.scalar.copy(dx[:, kt, 2 * pair * C : 2 * (pair + 1) * C], acc[:])
+
+        T_AHEAD, S_AHEAD, G_AHEAD = 3, 2, 2
+
+        def prepare(c, step):
+            if step == "act" and c < DIRECT:
+                direct_activations(c)
+            if step == "act" and DIRECT <= c <= last:
+                tanh_turned(c)
+            if step == "silu" and DIRECT <= c <= last:
+                silu(c)
+
+        def half(c, h, direct, turned):
+            if c < DIRECT:
+                if h == 0:
+                    direct(c)
+            elif c <= last:
+                bl = list(blocks(c))
+                for b in bl[:1] if h == 0 else bl[1:]:
+                    turned(c, b)
+
+        for c in range(-T_AHEAD, last + 1):
+            if c + S_AHEAD >= 0:
+                prepare(c + S_AHEAD, "silu")
+            prepare(c + T_AHEAD, "act")
+            if c >= 0:
+                gather(c, 0)
+            if c + 1 >= 0:
+                half(c + 1, 0, direct_factor, factor)
+            if c >= 0:
+                gather(c, 1)
+            if c + G_AHEAD >= 0:
+                half(c + G_AHEAD, 0, direct_gated, gated)
             if c > 0:
                 quantise(c - 1)
                 expert(c - 1)
-            gather(c, 2)
-            for b in ahead[1:]:
-                factor(c + 1, b)
-            for b in two_ahead[1:]:
-                gated(c + 2, b)
-            gather(c, 3)
-            interleave(c)
+            if c >= 0:
+                gather(c, 2)
+            if c + 1 >= 0:
+                half(c + 1, 1, direct_factor, factor)
+            if c + G_AHEAD >= 0:
+                half(c + G_AHEAD, 1, direct_gated, gated)
+            if c >= 0:
+                gather(c, 3)
+                interleave(c)
+            if c > 0:
+                collect(c - 1)
         quantise(last)
         expert(last)
+        collect(last)
 
         for kt in range(KT):
             got = [keep.tile([P, T], F32, name="got%d_%d" % (kt, r)) for r in range(TOP)]
             res = keep.tile([P, T], F32, name="res%d" % kt)
             if kt < KT - 1:
-                turned = [bank(b) for b in range(T // P)]
+                for later in [[1, 2], [3], []][kt]:
+                    if later >= EARLY:
+                        later_rows(later)
+                turned = [bank(b) for b in [[[0, 1, 4, 5], 6], [[0, 1, 4, 5], 7], [[0, 1, 4, 5], 6]][kt][0]]
                 for r in range(TOP):
                     nc.vector.tensor_copy(got[r][:], dx[:, kt, :].indirect(pos_sb[r][:]))
                     for b in range(T // P):
@@ -293,7 +331,7 @@ def tile_moe_sdb_silu_kernel(
                             is_transpose=True,
                         )
                 turned_sb = keep.tile([P, T], F32, name="turned%d" % kt)
-                back = bank(4 + kt % 2)
+                back = bank([[[0, 1, 4, 5], 6], [[0, 1, 4, 5], 7], [[0, 1, 4, 5], 6]][kt][1])
                 for b in range(T // P):
                     nc.scalar.copy(turned_sb[:, b * P : (b + 1) * P], turned[b][:, 0:P])
                     nc.tensor.transpose(back[:, b * P : (b + 1) * P], turned_sb[:, b * P : (b + 1) * P], ident[:])

from contextlib import ExitStack

import concourse.mybir as mybir
from concourse.masks import make_identity

K, T, E, C, H, N, TOP = 512, 512, 6, 256, 512, 1536, 3
S = E * C
FLOPS = 2 * N * H * T + 2 * H * K * S

F32 = mybir.dt.float32
BF16 = mybir.dt.bfloat16
I32 = mybir.dt.int32
U32 = mybir.dt.uint32
U16 = mybir.dt.uint16
U8 = mybir.dt.uint8
FP8X4 = mybir.dt.float8_e4m3fn_x4
FP4X4 = mybir.dt.float4_e2m1fn_x4
ACT = mybir.ActivationFunctionType
ALU = mybir.AluOpType

P = 128
PACK = 4
PASSES = N // (P * PACK)
KT = K // P
CHUNKS = [(0, 256), (256, 256), (512, 256), (768, 256), (1024, 256), (1280, 128), (1408, 128)]
GATED_ON_SCALAR = (3, 4, 5)
DIRECT = 3
EARLY = 1
CAST_ON_VECTOR = (6,)


def tile_moe_sdb_silu_kernel(
    tc, dy_words, dy_scales, w2t_words, w2t_scales, w1t_words, w1t_scales, a, gate, offs, pos1, pos2, pos3, out
):
    nc = tc.nc
    with ExitStack() as ctx:
        lists = ctx.enter_context(tc.tile_pool(name="lists", bufs=1))
        keep = ctx.enter_context(tc.tile_pool(name="keep", bufs=1))
        ring = ctx.enter_context(tc.tile_pool(name="ring", bufs=3))
        psum = ctx.enter_context(tc.psum_pool(name="psum", bufs=1))

        def bank(b):
            return psum.tile([P, 512], F32, name="bank%d" % b, tag="bank%d" % b)

        def load_scale_rows(queue, plane, rows):
            for q in range(4):
                queue.dma_start(
                    out=plane[32 * q : 32 * q + 4, :, :].bitcast(I32),
                    in_=rows[:, 4 * q : 4 * q + 4, :].rearrange("s r n -> r s n").bitcast(I32),
                )

        w2_raw = keep.tile([P, PASSES, 2 * H], U8, name="w2_raw", align_bytes=64)
        w2_scale_raw = keep.tile([P, PASSES, H], U8, name="w2_scale_raw", align_bytes=64)
        w2 = keep.tile([P, PASSES, PACK, 2 * P], U8, name="w2", align_bytes=64)
        w2_scale = keep.tile([P, PASSES, PACK, P], U8, name="w2_scale", align_bytes=64)
        dy = keep.tile([P, PASSES, PACK * T], U8, name="dy", align_bytes=64)
        dy_scale = keep.tile([P, PASSES, T], U8, name="dy_scale", align_bytes=64)
        w1 = keep.tile([P, E, 2 * K], U8, name="w1", align_bytes=64)
        w1_scale = keep.tile([P, E, K], U8, name="w1_scale", align_bytes=64)
        gate_sb = keep.tile([P, DIRECT * C], F32, name="gate_sb")
        gate_rows = keep.tile([P, P], F32, name="gate_rows")
        gate_cols = keep.tile([P, S // P], F32, name="gate_cols")
        a_sb = [keep.tile([P, PACK, n], F32, name="a%d" % c) for c, (s0, n) in enumerate(CHUNKS)]
        dc = [keep.tile([P, T], F32, name="dc%d" % j) for j in range(PACK)]
        codes = keep.tile([P, S], U32, name="codes", align_bytes=64)
        code_scale = keep.tile([P, S], U8, name="code_scale", align_bytes=64)
        dx = keep.tile([P, KT, S], F32, name="dx", align_bytes=64)
        ident = keep.tile([P, P], F32, name="ident")
        warm = keep.tile([P, 8], F32, name="warm")
        warm_out = keep.tile([P, 8], F32, name="warm_out")
        offs_sb = lists.tile([P, S // 16], U16, name="offs_sb")
        pos_sb = [lists.tile([P, T // 16], U16, name="pos%d_sb" % r) for r in range(TOP)]

        nc.gpsimd.memset(w2_scale_raw[:].bitcast(I32), 0)
        nc.vector.memset(dy_scale[:].bitcast(I32), 0)
        nc.vector.memset(warm[:], 0.0)
        nc.scalar.activation(warm_out[:], warm[:], ACT.Silu)
        nc.gpsimd.memset(w1_scale[:].bitcast(I32), 0)

        a_rows = a.rearrange("(p j) s -> p j s", j=PACK)

        def load_chunk(c):
            s0, n = CHUNKS[c]
            nc.sync.dma_start(out=a_sb[c][:], in_=a_rows[:, :, s0 : s0 + n])

        def load_w1(e0, e1):
            nc.sync.dma_start(
                out=w1[:, e0:e1, :].bitcast(I32),
                in_=w1t_words[e0:e1, 0].rearrange("e p b -> p e b").bitcast(I32),
            )

        def load_w2(s0, s1):
            nc.sync.dma_start(
                out=w2_raw[:, s0:s1, :].bitcast(I32), in_=w2t_words[s0:s1].rearrange("s p b -> p s b").bitcast(I32)
            )

        def load_dy(s0, s1):
            nc.sync.dma_start(
                out=dy[:, s0:s1, :].bitcast(I32),
                in_=dy_words[s0:s1].rearrange("s p t d -> p s (t d)").bitcast(I32),
            )

        def load_gate(c0, c1):
            nc.sync.dma_start(out=gate_sb[:, c0 * C : c1 * C], in_=gate[:, c0 * C : c1 * C])

        load_w2(1, PASSES)
        load_chunk(0)
        load_w2(0, 1)
        load_scale_rows(nc.sync, w2_scale_raw, w2t_scales)
        load_gate(0, 1)
        load_chunk(1)
        load_dy(0, 1)
        load_scale_rows(nc.sync, dy_scale, dy_scales)
        load_gate(1, DIRECT)
        load_chunk(2)
        load_dy(1, 2)
        load_dy(2, 3)
        nc.sync.dma_start(offs_sb[:], offs)
        nc.sync.dma_start(out=gate_rows[:], in_=gate.rearrange("r (b c) -> (r b) c", c=P)[0:P, :])
        load_chunk(3)
        load_chunk(4)
        load_w1(0, E)
        load_chunk(5)
        load_chunk(6)
        load_scale_rows(nc.sync, w1_scale, w1t_scales[:, 0])
        for r, pos in enumerate((pos1, pos2, pos3)):
            nc.sync.dma_start(pos_sb[r][:], pos)
        make_identity(nc, ident[:])

        def permute_words(s0, s1):
            nc.vector.tensor_copy(
                out=w2[:, s0:s1].bitcast(U16),
                in_=w2_raw[:, s0:s1].bitcast(U16).rearrange("p s (m j) -> p s j m", j=PACK),
            )

        permute_words(0, 1)
        nc.vector.tensor_copy(
            out=w2_scale[:].rearrange("p s j m -> p j s m"),
            in_=w2_scale_raw[:].rearrange("p s (m j) -> p j s m", j=PACK),
        )
        permute_words(1, PASSES)
        for j in range(PACK):
            acc = bank(j)
            order = [0, 1, 2] if j == 0 else [2, 0, 1]
            for s in order:
                nc.tensor.matmul_mx(
                    out=acc[:],
                    lhsT=w2[:, s, j, :].bitcast(FP4X4),
                    lhsT_scale=w2_scale[:, s, j, :],
                    rhs=dy[:, s, :].bitcast(FP8X4),
                    rhs_scale=dy_scale[:, s, :],
                    start=(s == order[0]),
                    stop=(s == order[-1]),
                )
            nc.scalar.activation(dc[j][:], acc[:], ACT.Copy, scale=-0.5)

        last = len(CHUNKS) - 1
        th, x, w, f, g, da, sums = {}, {}, {}, {}, {}, {}, {}

        gate_turned = bank(6)
        nc.tensor.transpose(gate_turned[:, 0:P], gate_rows[:], ident[:])
        nc.scalar.copy(gate_cols[:], gate_turned[:, 0 : S // P])

        def blocks(c):
            s0, n = CHUNKS[c]
            return range(s0 // P, (s0 + n) // P)

        def columns(c, b):
            return slice(b * P - CHUNKS[c][0], (b + 1) * P - CHUNKS[c][0])

        def silu(c):
            w[c] = keep.tile([P, PACK, CHUNKS[c][1]], F32, name="silu%d" % c)
            nc.scalar.activation(w[c][:], a_sb[c][:], ACT.Silu, scale=-1.0)
            f[c] = ring.tile([P, PACK, CHUNKS[c][1]], F32, name="f", tag="f", bufs=2)

        def tanh_turned(c):
            for b in blocks(c):
                turned = bank(4 + b % 2)
                for j in range(PACK):
                    nc.tensor.transpose(turned[:, j * P : (j + 1) * P], a_sb[c][:, j, columns(c, b)], ident[:])
                th[b] = keep.tile([P, H], F32, name="th%d" % b)
                nc.scalar.activation(th[b][:], turned[:], ACT.Tanh, scale=0.5)

        def gated(c, b):
            col = gate_cols[:, b : b + 1]
            y = ring.tile([P, H], F32, name="y", tag="y", bufs=3)
            if c in GATED_ON_SCALAR:
                nc.scalar.activation(y[:], th[b][:], ACT.Identity, bias=col, scale=col)
            else:
                nc.vector.tensor_scalar(y[:], th[b][:], col, col, ALU.mult, ALU.add)
            x[b] = bank(6 + b % 2)
            for j in range(PACK):
                nc.tensor.transpose(x[b][:, j * P : (j + 1) * P], y[:, j * P : (j + 1) * P], ident[:])

        def factor(c, b):
            cols = columns(c, b)
            nc.vector.scalar_tensor_tensor(
                f[c][:, :, cols], w[c][:, :, cols], -1.0, x[b][:].rearrange("p (j s) -> p j s", j=PACK), ALU.add, ALU.mult
            )

        def direct_activations(c):
            th[c, "direct"] = keep.tile([P, PACK, C], F32, name="th_direct%d" % c)
            nc.scalar.activation(th[c, "direct"][:], a_sb[c][:], ACT.Tanh, scale=0.5)
            silu(c)

        def direct_gated(c):
            gates = gate_sb[:, c * C : (c + 1) * C].unsqueeze(1).to_broadcast([P, PACK, C])
            nc.vector.scalar_tensor_tensor(th[c, "direct"][:], th[c, "direct"][:], 1.0, gates, ALU.add, ALU.mult)

        def direct_factor(c):
            nc.vector.scalar_tensor_tensor(f[c][:], w[c][:], -1.0, th[c, "direct"][:], ALU.add, ALU.mult)

        def gather(c, j):
            s0, n = CHUNKS[c]
            if j == 0:
                g[c] = ring.tile([P, PACK, n], F32, name="g", tag="g", bufs=4)
            window = dc[j][:].indirect(offs_sb[:, s0 // 16 : (s0 + n) // 16])
            nc.vector.tensor_tensor(g[c][:, j, :], window, f[c][:, j, :], ALU.mult)

        def interleave(c):
            n = CHUNKS[c][1]
            da[c] = ring.tile([P, PACK * n], BF16, name="da", tag="da", align_bytes=64)
            copy = nc.vector.tensor_copy if c in CAST_ON_VECTOR else nc.scalar.copy
            copy(
                da[c][:].rearrange("p (u i j) -> p u j i", i=4, j=PACK),
                g[c][:].rearrange("p j (u i) -> p u j i", i=4),
            )

        def quantise(c):
            s0, n = CHUNKS[c]
            nc.vector.quantize_mx(
                out=codes[:, s0 : s0 + n].bitcast(FP8X4), scales=code_scale[:, s0 : s0 + n], in_=da[c][:]
            )

        def product(acc, kt, s0, n):
            e = s0 // C
            nc.tensor.matmul_mx(
                out=acc,
                lhsT=w1[:, e, 2 * P * kt : 2 * P * (kt + 1)].bitcast(FP4X4),
                lhsT_scale=w1_scale[:, e, P * kt : P * (kt + 1)],
                rhs=codes[:, s0 : s0 + n].bitcast(FP8X4),
                rhs_scale=code_scale[:, s0 : s0 + n],
                start=True,
                stop=True,
            )

        def expert(c):
            s0, n = CHUNKS[c]
            sums[c] = bank(c % 2)
            for kt in range(EARLY):
                product(sums[c][:, kt * n : (kt + 1) * n], kt, s0, n)

        def collect(c):
            s0, n = CHUNKS[c]
            copy = nc.vector.tensor_copy if c == last else nc.scalar.copy
            copy(dx[:, 0:EARLY, s0 : s0 + n], sums[c][:, 0 : EARLY * n].rearrange("p (u s) -> p u s", u=EARLY))

        def later_rows(kt):
            for pair in range(E // 2):
                acc = bank([2, 3, 6, 7][(3 * kt + pair) % len([2, 3, 6, 7])])
                for u in range(2):
                    product(acc[:, u * C : (u + 1) * C], kt, (2 * pair + u) * C, C)
                nc.scalar.copy(dx[:, kt, 2 * pair * C : 2 * (pair + 1) * C], acc[:])

        T_AHEAD, S_AHEAD, G_AHEAD = 3, 2, 2

        def prepare(c, step):
            if step == "act" and c < DIRECT:
                direct_activations(c)
            if step == "act" and DIRECT <= c <= last:
                tanh_turned(c)
            if step == "silu" and DIRECT <= c <= last:
                silu(c)

        def half(c, h, direct, turned):
            if c < DIRECT:
                if h == 0:
                    direct(c)
            elif c <= last:
                bl = list(blocks(c))
                for b in bl[:1] if h == 0 else bl[1:]:
                    turned(c, b)

        for c in range(-T_AHEAD, last + 1):
            if c + S_AHEAD >= 0:
                prepare(c + S_AHEAD, "silu")
            prepare(c + T_AHEAD, "act")
            if c >= 0:
                gather(c, 0)
            if c + 1 >= 0:
                half(c + 1, 0, direct_factor, factor)
            if c >= 0:
                gather(c, 1)
            if c + G_AHEAD >= 0:
                half(c + G_AHEAD, 0, direct_gated, gated)
            if c > 0:
                quantise(c - 1)
                expert(c - 1)
            if c >= 0:
                gather(c, 2)
            if c + 1 >= 0:
                half(c + 1, 1, direct_factor, factor)
            if c + G_AHEAD >= 0:
                half(c + G_AHEAD, 1, direct_gated, gated)
            if c >= 0:
                gather(c, 3)
                interleave(c)
            if c > 0:
                collect(c - 1)
        quantise(last)
        expert(last)
        collect(last)

        for kt in range(KT):
            got = [keep.tile([P, T], F32, name="got%d_%d" % (kt, r)) for r in range(TOP)]
            res = keep.tile([P, T], F32, name="res%d" % kt)
            if kt < KT - 1:
                for later in [[1, 2], [3], []][kt]:
                    if later >= EARLY:
                        later_rows(later)
                turned = [bank(b) for b in [[[0, 1, 4, 5], 6], [[0, 1, 4, 5], 7], [[0, 1, 4, 5], 6]][kt][0]]
                for r in range(TOP):
                    nc.vector.tensor_copy(got[r][:], dx[:, kt, :].indirect(pos_sb[r][:]))
                    for b in range(T // P):
                        nc.tensor.matmul(
                            turned[b][:, 0:P],
                            lhsT=got[r][:, b * P : (b + 1) * P],
                            rhs=ident[:],
                            start=(r == 0),
                            stop=(r == TOP - 1),
                            is_transpose=True,
                        )
                turned_sb = keep.tile([P, T], F32, name="turned%d" % kt)
                back = bank([[[0, 1, 4, 5], 6], [[0, 1, 4, 5], 7], [[0, 1, 4, 5], 6]][kt][1])
                for b in range(T // P):
                    nc.scalar.copy(turned_sb[:, b * P : (b + 1) * P], turned[b][:, 0:P])
                    nc.tensor.transpose(back[:, b * P : (b + 1) * P], turned_sb[:, b * P : (b + 1) * P], ident[:])
                nc.scalar.copy(res[:], back[:])
                nc.sync.dma_start(out=out[kt * P : (kt + 1) * P, :], in_=res[:])
            else:
                pair = keep.tile([P, T], F32, name="pair")
                for r in range(2):
                    nc.vector.tensor_copy(got[r][:], dx[:, kt, :].indirect(pos_sb[r][:]))
                halves = [slice(0, T // 2), slice(T // 2, T)]
                nc.vector.tensor_copy(got[2][:, halves[0]], dx[:, kt, :].indirect(pos_sb[2][:, 0:16]))
                nc.vector.tensor_tensor(pair[:], got[0][:], got[1][:], ALU.add)
                nc.vector.tensor_copy(got[2][:, halves[1]], dx[:, kt, :].indirect(pos_sb[2][:, 16:32]))
                for h in halves:
                    nc.vector.tensor_tensor(res[:, h], pair[:, h], got[2][:, h], ALU.add)
                    nc.sync.dma_start(out=out[kt * P : (kt + 1) * P, h], in_=res[:, h])
